import numpy as np
import ml_dtypes


def mxq(x, axis, fmt="e4m3"):
    dtype, down = {"e4m3": (ml_dtypes.float8_e4m3fn, 7), "e5m2": (ml_dtypes.float8_e5m2, 14)}[fmt]
    v = np.moveaxis(np.asarray(x, np.float32).astype(ml_dtypes.bfloat16).astype(np.float64), axis, -1)
    blocks = v.reshape(v.shape[:-1] + (-1, 32))
    amax = np.abs(blocks).max(-1, keepdims=True)
    byte = np.maximum(np.where(amax > 0, np.frexp(amax)[1] - 1 + 127, 0) - down, 1)
    scale = np.exp2(byte - 127.0)
    codes = (blocks / scale).astype(np.float32).astype(dtype).astype(np.float64)
    return np.moveaxis((codes * scale).reshape(v.shape), -1, axis)


WIDE = False


def mx_kscale(k):
    if not WIDE:
        return np.ones(k)
    levels = np.array([10, -10, 5, -5, 0])
    if k % 512:
        return np.exp2(np.random.permutation(np.resize(levels, k // 32))).repeat(32)
    a = np.empty((k // 512, 16))
    for p in range(k // 512):
        a[p, :8] = np.random.permutation(np.resize(levels, 8))
        for g in range(8):
            far = levels[np.abs(levels - a[p, g]) >= 10]
            a[p, g + 8] = far[np.random.randint(len(far))]
    return np.exp2(a.ravel()).repeat(32)


def f64(x):
    return np.asarray(x).astype(np.float64)


def striped(idx):
    return np.tile(idx.reshape(-1, 16).T, (8, 1)).astype(np.uint16)


def unstriped(offs):
    return offs[:16].T.reshape(-1).astype(np.int64)


def striped8(idx):
    return np.concatenate([v.reshape(-1, 16).T for v in idx]).astype(np.uint16)


def unstriped8(offs):
    return np.stack([offs[16 * g:16 * g + 16].T.reshape(-1) for g in range(8)]).astype(np.int64)


E2M1 = np.array([0.0, 0.5, 1.0, 1.5, 2.0, 3.0, 4.0, 6.0, -0.0, -0.5, -1.0, -1.5, -2.0, -3.0, -4.0, -6.0])


def pack_weight(w, fmt):
    k, n = w.shape
    w = f64(np.asarray(w, np.float32).astype(ml_dtypes.bfloat16)).reshape(k // 32, 32, n)
    amax = np.abs(w).max(1)
    if fmt == "e4m3":
        byte = np.frexp(amax)[1] - 1 + 127 - 7
    else:
        mant, ex = np.frexp(amax / 6.0)
        byte = np.where(mant > 0.5, ex, ex - 1) + 127
    byte = np.clip(np.where(amax > 0, byte, 1), 1, 254)
    scaled = (w * np.exp2(127.0 - byte)[:, None, :]).reshape(k, n).astype(np.float32)
    by_word = np.ascontiguousarray(scaled.reshape(k // 512, 128, 4, n).transpose(0, 1, 3, 2))
    if fmt == "e4m3":
        words = by_word.astype(ml_dtypes.float8_e4m3fn).view(np.uint8)
    else:
        c = by_word.astype(ml_dtypes.float4_e2m1fn).view(np.uint8) & 0xF
        words = (c[..., 0::2] | (c[..., 1::2] << 4)).reshape(k // 512, 128, 2 * n)
    return np.ascontiguousarray(words), np.ascontiguousarray(byte.astype(np.uint8).reshape(k // 512, 16, n))


def unpack_weight(words, scales, fmt):
    g, _, n = scales.shape
    words = np.ascontiguousarray(words).reshape(g, 128, n, -1)
    if fmt == "e4m3":
        vals = words.view(ml_dtypes.float8_e4m3fn).astype(np.float64)
    else:
        nib = np.empty((g, 128, n, 4), np.uint8)
        nib[..., 0::2] = words & 0xF
        nib[..., 1::2] = words >> 4
        vals = E2M1[nib]
    vals = vals * np.repeat(np.exp2(scales.astype(np.float64) - 127.0), 8, axis=1)[..., None]
    return vals.transpose(0, 1, 3, 2).reshape(g * 512, n)


def pack_table(v):
    words, scales = pack_weight(v, "e4m3")
    return np.concatenate([words.reshape(words.shape[0], -1), scales.reshape(scales.shape[0], -1)], axis=1)


def unpack_table(tab):
    g, t = tab.shape[0], tab.shape[1] // 528
    return unpack_weight(tab[:, :512 * t].reshape(g, 128, t, 4), tab[:, 512 * t:].reshape(g, 16, t), "e4m3")


def gelu(v):
    return 0.5 * v * (1.0 + np.tanh(np.sqrt(2.0 / np.pi) * (v + 0.044715 * v**3)))


K, M, T, S = 2048, 256, 2048, 1024


def setup_inputs():
    n = np.random.standard_normal
    s = mx_kscale(K)[:, None]
    u = mx_kscale(512)[:, None]
    p_w2 = pack_weight(1.4 * n((512, M)) / np.sqrt(512) / u, "e2m1")
    return {
        "tab": pack_table(n((K, T)) * s),
        "w1": (n((K, 512)) / np.sqrt(K) / s * u.T).astype(np.float32),
        "w2_words": p_w2[0],
        "w2_scales": p_w2[1],
        "b": (0.3 * n(256)).astype(np.float32),
        "wgo": np.repeat(np.random.uniform(0.5, 2.0, (8, S)), 16, axis=0).astype(np.float32),
        "offs": striped(np.random.permutation(T)[:S]),
        "offs2": striped8(np.stack([np.random.permutation(T)[:S] for _ in range(8)])),
    }


def reference(tab, w1, w2_words, w2_scales, b, wgo, offs, offs2):
    tab_ = unpack_table(tab)[:, unstriped(offs)]
    w1_ = mxq(f64(w1), 0, "e4m3")
    w2_ = unpack_weight(w2_words, w2_scales, "e2m1")
    h_ = mxq(np.maximum(w1_.T @ tab_, 0.0), 0, "e4m3")
    y = w2_.T @ h_
    place = unstriped8(offs2)[np.arange(M) % 128 // 16]
    out = np.zeros((M, T))
    out[np.arange(M)[:, None], place] = f64(wgo)[np.arange(M) % 128] * (gelu(y + f64(b)[:, None]))
    return out

@@ -1,0 +1,201 @@
+from contextlib import ExitStack
+
+import concourse.mybir as mybir
+
+K, M, T, S, H = 2048, 256, 2048, 1024, 512
+FLOPS = 2 * K * H * S + 2 * H * M * S
+
+F32 = mybir.dt.float32
+BF16 = mybir.dt.bfloat16
+I32 = mybir.dt.int32
+U32 = mybir.dt.uint32
+U16 = mybir.dt.uint16
+U8 = mybir.dt.uint8
+FP8X4 = mybir.dt.float8_e4m3fn_x4
+FP4X4 = mybir.dt.float4_e2m1fn_x4
+ACT = mybir.ActivationFunctionType
+MULT = mybir.AluOpType.mult
+
+P = 128
+PACK = 4
+PASSES = K // (P * PACK)
+SLICE = 128
+SLICES = S // SLICE
+PER_COL = 16
+SCALAR_SHARE = 48
+
+
+def tile_list_tabhs_m_gelu_kernel(tc, tab, w1, w2_words, w2_scales, b, wgo, offs, offs2, out):
+    nc = tc.nc
+    last = PASSES - 1
+    with ExitStack() as ctx:
+        keep = ctx.enter_context(tc.tile_pool(name="keep", bufs=1))
+        psum = ctx.enter_context(tc.psum_pool(name="psum", bufs=1))
+
+        pick = keep.tile([P, S // PER_COL], U16, name="pick")
+        place = keep.tile([P, S // PER_COL], U16, name="place")
+        tab_words = [keep.tile([P, T], I32, name=f"tab_words{a}") for a in range(PASSES)]
+        tab_scales = keep.tile([P, T], U8, name="tab_scales")
+        w1_raw = [keep.tile([P, PACK, H], F32, name=f"w1_raw{a}") for a in range(PASSES)]
+        w2w = keep.tile([P, 2 * M], U8, name="w2w", align_bytes=64)
+        w2s = keep.tile([P, M], U8, name="w2s", align_bytes=64)
+        bias = keep.tile([P, 2], F32, name="bias")
+        gain = keep.tile([P, S], F32, name="gain")
+        pages = [keep.tile([P, T], F32, name=f"page{c}") for c in range(2)]
+
+        def load_tab(a):
+            nc.sync.dma_start(out=tab_words[a][:], in_=tab[a, 0 : P * PACK * T].bitcast(I32).rearrange("(p t) -> p t", p=P))
+
+        def load_w1(a):
+            rows = w1[a * P * PACK : (a + 1) * P * PACK, :]
+            nc.sync.dma_start(out=w1_raw[a][:], in_=rows.rearrange("(p j) c -> p j c", j=PACK))
+
+        nc.vector.memset(tab_scales[:].bitcast(I32), 0)
+        nc.sync.dma_start(pick[:], offs)
+        load_tab(0)
+        for q in range(4):
+            first = P * PACK * T + 4 * q * T
+            rows = tab[:, first : first + 4 * T].bitcast(I32).rearrange("a (r w) -> a r w", r=4)
+            nc.sync.dma_start(out=tab_scales[32 * q : 32 * q + 16, :].bitcast(I32), in_=rows)
+        load_w1(0)
+        for a in range(1, PASSES):
+            load_w1(a)
+            load_tab(a)
+        nc.sync.dma_start(out=w2w[:].bitcast(I32), in_=w2_words[0].bitcast(I32))
+        with nc.allow_non_contiguous_dma("one bias value a partition and half"):
+            nc.sync.dma_start(out=bias[:], in_=b.rearrange("(c p) -> p c", p=P))
+        nc.sync.dma_start(place[:], offs2)
+        nc.sync.dma_start(out=gain[:], in_=wgo)
+
+        nc.gpsimd.memset(w2s[:].bitcast(I32), 0)
+        for q in range(4):
+            nc.gpsimd.dma_start(out=w2s[32 * q : 32 * q + 4, :].bitcast(I32), in_=w2_scales[0, 4 * q : 4 * q + 4, :].bitcast(I32))
+
+        warm = keep.tile([P, 2], F32, name="warm")
+        nc.vector.memset(warm[:, 0:1], 0.0)
+        nc.scalar.activation(out=warm[:, 1:2], in_=warm[:, 0:1], func=ACT.Gelu_apprx_tanh)
+        for c in range(2):
+            nc.vector.memset(pages[c][:], 0.0)
+
+        picked = {}
+
+        def gather_words(a, j0, n):
+            got = keep.tile([P, n], U32, name=f"got{a}_{j0}", align_bytes=64)
+            window = tab_words[a][:].bitcast(U32)
+            nc.vector.tensor_copy(got[:], window.indirect(pick[:, j0 // PER_COL : (j0 + n) // PER_COL]))
+            for s in range(j0 // SLICE, (j0 + n) // SLICE):
+                picked[(a, s)] = got[:, s * SLICE - j0 : (s + 1) * SLICE - j0]
+
+        w1_codes = [keep.tile([P, H], U32, name=f"w1_codes{a}", align_bytes=64) for a in range(PASSES)]
+        w1_scales = [keep.tile([P, H], U8, name=f"w1_scales{a}", align_bytes=64) for a in range(PASSES)]
+
+        def quantise_w1(a):
+            woven = keep.tile([P, PACK * H], BF16, name=f"woven{a}", align_bytes=64)
+            dst = woven[:].rearrange("p (t m j) -> p m j t", t=PACK, j=PACK)
+            src = w1_raw[a][:].rearrange("p j (m t) -> p m j t", t=PACK)
+            if a == last:
+                nc.scalar.copy(out=dst[:, 0:SCALAR_SHARE], in_=src[:, 0:SCALAR_SHARE])
+                nc.vector.tensor_copy(out=dst[:, SCALAR_SHARE:P], in_=src[:, SCALAR_SHARE:P])
+            else:
+                nc.scalar.copy(out=dst, in_=src)
+            nc.vector.quantize_mx(out=w1_codes[a][:].bitcast(FP8X4), scales=w1_scales[a][:], in_=woven[:])
+
+        got_scales = keep.tile([P, S], U8, name="got_scales", align_bytes=64)
+        h_banks = [psum.tile([P, PACK, SLICE], F32, name=f"h{s}", tag=f"bank{s}") for s in range(SLICES)]
+
+        def first_product(a, s):
+            for t in range(PACK):
+                cols = slice(t * P, (t + 1) * P)
+                nc.tensor.matmul_mx(
+                    out=h_banks[s][:, t, :],
+                    lhsT=w1_codes[a][:, cols].bitcast(FP8X4),
+                    lhsT_scale=w1_scales[a][:, cols],
+                    rhs=picked[(a, s)].bitcast(FP8X4),
+                    rhs_scale=got_scales[4 * a : P, s * SLICE : (s + 1) * SLICE],
+                    start=(a == 0 and t == 0),
+                    stop=(a == last and t == PACK - 1),
+                )
+
+        for a in range(last):
+            for half in range(2):
+                gather_words(a, half * (S // 2), S // 2)
+            if a == 0:
+                nc.vector.tensor_copy(got_scales[:], tab_scales[:].indirect(pick[:]))
+            quantise_w1(a)
+            for s in range(SLICES):
+                first_product(a, s)
+        quantise_w1(last)
+        for j0 in range(0, S, 2 * SLICE):
+            gather_words(last, j0, 2 * SLICE)
+
+        groups = [(0, 1), (1, 2), (2, 4), (4, 8)]
+        h_bf = {}
+        h_codes = {}
+        h_scales = {}
+        y_banks = {}
+        for s0, s1 in groups:
+            n = (s1 - s0) * SLICE
+            h_bf[s0] = keep.tile([P, PACK * n], BF16, name=f"h_bf{s0}", align_bytes=64)
+            h_codes[s0] = keep.tile([P, n], U32, name=f"h_codes{s0}", align_bytes=64)
+            h_scales[s0] = keep.tile([P, n], U8, name=f"h_scales{s0}", align_bytes=64)
+
+        def relu(s0, s):
+            first_product(last, s)
+            lo = (s - s0) * PACK * SLICE
+            dst = h_bf[s0][:, lo : lo + PACK * SLICE].rearrange("p (n t) -> p n t", t=PACK)
+            nc.scalar.activation(out=dst, in_=h_banks[s][:].rearrange("p t n -> p n t"), func=ACT.Relu)
+
+        def quantise_h(s0):
+            nc.vector.quantize_mx(out=h_codes[s0][:].bitcast(FP8X4), scales=h_scales[s0][:], in_=h_bf[s0][:])
+
+        def second_product(s0, s1):
+            n = (s1 - s0) * SLICE
+            if s1 - s0 == 1:
+                both = psum.tile([P, 2, n], F32, name=f"y{s0}", tag=f"bank{s0}")
+                outs = [both[:, 0, :], both[:, 1, :]]
+            else:
+                outs = [psum.tile([P, n], F32, name=f"y{s0}_{c}", tag=f"bank{s0 + c}")[:] for c in range(2)]
+            for c in range(2):
+                nc.tensor.matmul_mx(
+                    out=outs[c],
+                    lhsT=w2w[:, 2 * P * c : 2 * P * (c + 1)].bitcast(FP4X4),
+                    lhsT_scale=w2s[:, P * c : P * (c + 1)],
+                    rhs=h_codes[s0][:].bitcast(FP8X4),
+                    rhs_scale=h_scales[s0][:],
+                    start=True,
+                    stop=True,
+                )
+                y_banks[(s0, c)] = outs[c]
+
+        def put(s0, s1, c):
+            j0, j1 = s0 * SLICE, s1 * SLICE
+            act = keep.tile([P, j1 - j0], F32, name=f"act{s0}_{c}")
+            nc.scalar.activation(out=act[:], in_=y_banks[(s0, c)], func=ACT.Gelu_apprx_tanh, bias=bias[:, c : c + 1])
+            window = pages[c][:].indirect(place[:, j0 // PER_COL : j1 // PER_COL])
+            nc.vector.tensor_tensor(window, act[:], gain[:, j0:j1], MULT)
+
+        relu(0, 0)
+        quantise_h(0)
+        relu(1, 1)
+        quantise_h(1)
+        second_product(0, 1)
+        put(0, 1, 0)
+        put(0, 1, 1)
+        relu(2, 2)
+        relu(2, 3)
+        quantise_h(2)
+        second_product(1, 2)
+        put(1, 2, 0)
+        put(1, 2, 1)
+        relu(4, 4)
+        relu(4, 5)
+        second_product(2, 4)
+        put(2, 4, 0)
+        relu(4, 6)
+        relu(4, 7)
+        quantise_h(4)
+        put(2, 4, 1)
+        second_product(4, 8)
+        for c in range(2):
+            put(4, 8, c)
+            nc.sync.dma_start(out=out[c * P : (c + 1) * P, :], in_=pages[c][:])

@@ -22,7 +22,6 @@ PASSES = K // (P * PACK)
 SLICE = 128
 SLICES = S // SLICE
 PER_COL = 16
-SCALAR_SHARE = 48
 
 
 def tile_list_tabhs_m_gelu_kernel(tc, tab, w1, w2_words, w2_scales, b, wgo, offs, offs2, out):
@@ -51,8 +50,9 @@ def tile_list_tabhs_m_gelu_kernel(tc, tab, w1, w2_words, w2_scales, b, wgo, offs
             nc.sync.dma_start(out=w1_raw[a][:], in_=rows.rearrange("(p j) c -> p j c", j=PACK))
 
         nc.vector.memset(tab_scales[:].bitcast(I32), 0)
-        nc.sync.dma_start(pick[:], offs)
+        nc.vector.memset(w2s[:].bitcast(I32), 0)
         load_tab(0)
+        nc.sync.dma_start(pick[:], offs)
         for q in range(4):
             first = P * PACK * T + 4 * q * T
             rows = tab[:, first : first + 4 * T].bitcast(I32).rearrange("a (r w) -> a r w", r=4)
@@ -61,15 +61,14 @@ def tile_list_tabhs_m_gelu_kernel(tc, tab, w1, w2_words, w2_scales, b, wgo, offs
         for a in range(1, PASSES):
             load_w1(a)
             load_tab(a)
-        nc.sync.dma_start(out=w2w[:].bitcast(I32), in_=w2_words[0].bitcast(I32))
-        with nc.allow_non_contiguous_dma("one bias value a partition and half"):
-            nc.sync.dma_start(out=bias[:], in_=b.rearrange("(c p) -> p c", p=P))
+            if a == 1:
+                nc.sync.dma_start(out=w2w[:].bitcast(I32), in_=w2_words[0].bitcast(I32))
+                for q in range(4):
+                    nc.sync.dma_start(out=w2s[32 * q : 32 * q + 4, :].bitcast(I32), in_=w2_scales[0, 4 * q : 4 * q + 4, :].bitcast(I32))
+                with nc.allow_non_contiguous_dma("one bias value a partition and half"):
+                    nc.sync.dma_start(out=bias[:], in_=b.rearrange("(c p) -> p c", p=P))
         nc.sync.dma_start(place[:], offs2)
         nc.sync.dma_start(out=gain[:], in_=wgo)
-
-        nc.gpsimd.memset(w2s[:].bitcast(I32), 0)
-        for q in range(4):
-            nc.gpsimd.dma_start(out=w2s[32 * q : 32 * q + 4, :].bitcast(I32), in_=w2_scales[0, 4 * q : 4 * q + 4, :].bitcast(I32))
 
         warm = keep.tile([P, 2], F32, name="warm")
         nc.vector.memset(warm[:, 0:1], 0.0)
@@ -79,8 +78,8 @@ def tile_list_tabhs_m_gelu_kernel(tc, tab, w1, w2_words, w2_scales, b, wgo, offs
 
         picked = {}
 
-        def gather_words(a, j0, n):
-            got = keep.tile([P, n], U32, name=f"got{a}_{j0}", align_bytes=64)
+        def gather_words(a, j0, n, tag=""):
+            got = keep.tile([P, n], U32, name=f"got{a}_{j0}", tag=tag, align_bytes=64)
             window = tab_words[a][:].bitcast(U32)
             nc.vector.tensor_copy(got[:], window.indirect(pick[:, j0 // PER_COL : (j0 + n) // PER_COL]))
             for s in range(j0 // SLICE, (j0 + n) // SLICE):
@@ -93,12 +92,17 @@ def tile_list_tabhs_m_gelu_kernel(tc, tab, w1, w2_words, w2_scales, b, wgo, offs
             woven = keep.tile([P, PACK * H], BF16, name=f"woven{a}", align_bytes=64)
             dst = woven[:].rearrange("p (t m j) -> p m j t", t=PACK, j=PACK)
             src = w1_raw[a][:].rearrange("p j (m t) -> p m j t", t=PACK)
-            if a == last:
-                nc.scalar.copy(out=dst[:, 0:SCALAR_SHARE], in_=src[:, 0:SCALAR_SHARE])
-                nc.vector.tensor_copy(out=dst[:, SCALAR_SHARE:P], in_=src[:, SCALAR_SHARE:P])
+            if a >= last - 1:
+                nc.vector.tensor_copy(out=dst[:, :, :, 0:2], in_=src[:, :, :, 0:2])
+                nc.scalar.copy(out=dst[:, :, :, 2:4], in_=src[:, :, :, 2:4])
+                for half in range(2):
+                    cols = slice(half * (H // 2), (half + 1) * (H // 2))
+                    wide = slice(half * PACK * (H // 2), (half + 1) * PACK * (H // 2))
+                    nc.vector.quantize_mx(out=w1_codes[a][:, cols].bitcast(FP8X4), scales=w1_scales[a][:, cols], in_=woven[:, wide])
             else:
-                nc.scalar.copy(out=dst, in_=src)
-            nc.vector.quantize_mx(out=w1_codes[a][:].bitcast(FP8X4), scales=w1_scales[a][:], in_=woven[:])
+                nc.scalar.copy(out=dst[:, :, :, 0:2], in_=src[:, :, :, 0:2])
+                nc.scalar.copy(out=dst[:, :, :, 2:4], in_=src[:, :, :, 2:4])
+                nc.vector.quantize_mx(out=w1_codes[a][:].bitcast(FP8X4), scales=w1_scales[a][:], in_=woven[:])
 
         got_scales = keep.tile([P, S], U8, name="got_scales", align_bytes=64)
         h_banks = [psum.tile([P, PACK, SLICE], F32, name=f"h{s}", tag=f"bank{s}") for s in range(SLICES)]
@@ -125,17 +129,16 @@ def tile_list_tabhs_m_gelu_kernel(tc, tab, w1, w2_words, w2_scales, b, wgo, offs
             for s in range(SLICES):
                 first_product(a, s)
         quantise_w1(last)
-        for j0 in range(0, S, 2 * SLICE):
+        for j0 in range(0, S - 2 * SLICE, 2 * SLICE):
             gather_words(last, j0, 2 * SLICE)
 
         groups = [(0, 1), (1, 2), (2, 4), (4, 8)]
         h_bf = {}
         h_codes = {}
         h_scales = {}
-        y_banks = {}
         for s0, s1 in groups:
             n = (s1 - s0) * SLICE
-            h_bf[s0] = keep.tile([P, PACK * n], BF16, name=f"h_bf{s0}", align_bytes=64)
+            h_bf[s0] = keep.tile([P, PACK * n], BF16, name=f"h_bf{s0}", tag=f"h_bf{s0}", align_bytes=64)
             h_codes[s0] = keep.tile([P, n], U32, name=f"h_codes{s0}", align_bytes=64)
             h_scales[s0] = keep.tile([P, n], U8, name=f"h_scales{s0}", align_bytes=64)
 
@@ -148,54 +151,44 @@ def tile_list_tabhs_m_gelu_kernel(tc, tab, w1, w2_words, w2_scales, b, wgo, offs
         def quantise_h(s0):
             nc.vector.quantize_mx(out=h_codes[s0][:].bitcast(FP8X4), scales=h_scales[s0][:], in_=h_bf[s0][:])
 
-        def second_product(s0, s1):
-            n = (s1 - s0) * SLICE
-            if s1 - s0 == 1:
-                both = psum.tile([P, 2, n], F32, name=f"y{s0}", tag=f"bank{s0}")
-                outs = [both[:, 0, :], both[:, 1, :]]
-            else:
-                outs = [psum.tile([P, n], F32, name=f"y{s0}_{c}", tag=f"bank{s0 + c}")[:] for c in range(2)]
-            for c in range(2):
-                nc.tensor.matmul_mx(
-                    out=outs[c],
-                    lhsT=w2w[:, 2 * P * c : 2 * P * (c + 1)].bitcast(FP4X4),
-                    lhsT_scale=w2s[:, P * c : P * (c + 1)],
-                    rhs=h_codes[s0][:].bitcast(FP8X4),
-                    rhs_scale=h_scales[s0][:],
-                    start=True,
-                    stop=True,
-                )
-                y_banks[(s0, c)] = outs[c]
+        def second_product(c, lo, hi, bank):
+            y = psum.tile([P, (hi - lo) * SLICE], F32, name=f"y{c}_{lo}", tag=f"bank{bank}")
+            for s0, s1 in groups:
+                if lo <= s0 and s1 <= hi:
+                    nc.tensor.matmul_mx(
+                        out=y[:, (s0 - lo) * SLICE : (s1 - lo) * SLICE],
+                        lhsT=w2w[:, 2 * P * c : 2 * P * (c + 1)].bitcast(FP4X4),
+                        lhsT_scale=w2s[:, P * c : P * (c + 1)],
+                        rhs=h_codes[s0][:].bitcast(FP8X4),
+                        rhs_scale=h_scales[s0][:],
+                        start=True,
+                        stop=True,
+                    )
+            return y
 
-        def put(s0, s1, c):
-            j0, j1 = s0 * SLICE, s1 * SLICE
-            act = keep.tile([P, j1 - j0], F32, name=f"act{s0}_{c}")
-            nc.scalar.activation(out=act[:], in_=y_banks[(s0, c)], func=ACT.Gelu_apprx_tanh, bias=bias[:, c : c + 1])
+        def put(c, lo, hi, y):
+            j0, j1 = lo * SLICE, hi * SLICE
+            act = keep.tile([P, j1 - j0], F32, name=f"act{c}_{lo}")
+            nc.scalar.activation(out=act[:], in_=y[:], func=ACT.Gelu_apprx_tanh, bias=bias[:, c : c + 1])
             window = pages[c][:].indirect(place[:, j0 // PER_COL : j1 // PER_COL])
             nc.vector.tensor_tensor(window, act[:], gain[:, j0:j1], MULT)
 
         relu(0, 0)
         quantise_h(0)
+        gather_words(last, S - 2 * SLICE, 2 * SLICE, tag="h_bf0")
         relu(1, 1)
         quantise_h(1)
-        second_product(0, 1)
-        put(0, 1, 0)
-        put(0, 1, 1)
+        y = second_product(0, 0, 1, 0)
         relu(2, 2)
+        put(0, 0, 1, y)
         relu(2, 3)
         quantise_h(2)
-        second_product(1, 2)
-        put(1, 2, 0)
-        put(1, 2, 1)
-        relu(4, 4)
-        relu(4, 5)
-        second_product(2, 4)
-        put(2, 4, 0)
-        relu(4, 6)
-        relu(4, 7)
+        put(1, 0, 2, second_product(1, 0, 2, 3))
+        put(0, 1, 4, second_product(0, 1, 4, 2))
+        for s in range(4, 8):
+            relu(4, s)
         quantise_h(4)
-        put(2, 4, 1)
-        second_product(4, 8)
+        put(1, 2, 4, second_product(1, 2, 4, 7))
         for c in range(2):
-            put(4, 8, c)
+            put(c, 4, 8, second_product(c, 4, 8, 4 + c))
             nc.sync.dma_start(out=out[c * P : (c + 1) * P, :], in_=pages[c][:])

from contextlib import ExitStack

import concourse.mybir as mybir

K, M, T, S, H = 2048, 256, 2048, 1024, 512
FLOPS = 2 * K * H * S + 2 * H * M * S

F32 = mybir.dt.float32
BF16 = mybir.dt.bfloat16
I32 = mybir.dt.int32
U32 = mybir.dt.uint32
U16 = mybir.dt.uint16
U8 = mybir.dt.uint8
FP8X4 = mybir.dt.float8_e4m3fn_x4
FP4X4 = mybir.dt.float4_e2m1fn_x4
ACT = mybir.ActivationFunctionType
MULT = mybir.AluOpType.mult

P = 128
PACK = 4
PASSES = K // (P * PACK)
SLICE = 128
SLICES = S // SLICE
PER_COL = 16


def tile_list_tabhs_m_gelu_kernel(tc, tab, w1, w2_words, w2_scales, b, wgo, offs, offs2, out):
    nc = tc.nc
    last = PASSES - 1
    with ExitStack() as ctx:
        keep = ctx.enter_context(tc.tile_pool(name="keep", bufs=1))
        psum = ctx.enter_context(tc.psum_pool(name="psum", bufs=1))

        pick = keep.tile([P, S // PER_COL], U16, name="pick")
        place = keep.tile([P, S // PER_COL], U16, name="place")
        tab_words = [keep.tile([P, T], I32, name=f"tab_words{a}") for a in range(PASSES)]
        tab_scales = keep.tile([P, T], U8, name="tab_scales")
        w1_raw = [keep.tile([P, PACK, H], F32, name=f"w1_raw{a}") for a in range(PASSES)]
        w2w = keep.tile([P, 2 * M], U8, name="w2w", align_bytes=64)
        w2s = keep.tile([P, M], U8, name="w2s", align_bytes=64)
        bias = keep.tile([P, 2], F32, name="bias")
        gain = keep.tile([P, S], F32, name="gain")
        pages = [keep.tile([P, T], F32, name=f"page{c}") for c in range(2)]

        def load_tab(a):
            nc.sync.dma_start(out=tab_words[a][:], in_=tab[a, 0 : P * PACK * T].bitcast(I32).rearrange("(p t) -> p t", p=P))

        def load_w1(a):
            rows = w1[a * P * PACK : (a + 1) * P * PACK, :]
            nc.sync.dma_start(out=w1_raw[a][:], in_=rows.rearrange("(p j) c -> p j c", j=PACK))

        nc.vector.memset(tab_scales[:].bitcast(I32), 0)
        nc.vector.memset(w2s[:].bitcast(I32), 0)
        load_tab(0)
        nc.sync.dma_start(pick[:], offs)
        for q in range(4):
            first = P * PACK * T + 4 * q * T
            rows = tab[:, first : first + 4 * T].bitcast(I32).rearrange("a (r w) -> a r w", r=4)
            nc.sync.dma_start(out=tab_scales[32 * q : 32 * q + 16, :].bitcast(I32), in_=rows)
        load_w1(0)
        for a in range(1, PASSES):
            load_w1(a)
            load_tab(a)
            if a == 1:
                nc.sync.dma_start(out=w2w[:].bitcast(I32), in_=w2_words[0].bitcast(I32))
                for q in range(4):
                    nc.sync.dma_start(out=w2s[32 * q : 32 * q + 4, :].bitcast(I32), in_=w2_scales[0, 4 * q : 4 * q + 4, :].bitcast(I32))
                with nc.allow_non_contiguous_dma("one bias value a partition and half"):
                    nc.sync.dma_start(out=bias[:], in_=b.rearrange("(c p) -> p c", p=P))
        nc.sync.dma_start(place[:], offs2)
        nc.sync.dma_start(out=gain[:], in_=wgo)

        warm = keep.tile([P, 2], F32, name="warm")
        nc.vector.memset(warm[:, 0:1], 0.0)
        nc.scalar.activation(out=warm[:, 1:2], in_=warm[:, 0:1], func=ACT.Gelu_apprx_tanh)
        for c in range(2):
            nc.vector.memset(pages[c][:], 0.0)

        picked = {}

        def gather_words(a, j0, n, tag=""):
            got = keep.tile([P, n], U32, name=f"got{a}_{j0}", tag=tag, align_bytes=64)
            window = tab_words[a][:].bitcast(U32)
            nc.vector.tensor_copy(got[:], window.indirect(pick[:, j0 // PER_COL : (j0 + n) // PER_COL]))
            for s in range(j0 // SLICE, (j0 + n) // SLICE):
                picked[(a, s)] = got[:, s * SLICE - j0 : (s + 1) * SLICE - j0]

        w1_codes = [keep.tile([P, H], U32, name=f"w1_codes{a}", align_bytes=64) for a in range(PASSES)]
        w1_scales = [keep.tile([P, H], U8, name=f"w1_scales{a}", align_bytes=64) for a in range(PASSES)]

        def quantise_w1(a):
            woven = keep.tile([P, PACK * H], BF16, name=f"woven{a}", align_bytes=64)
            dst = woven[:].rearrange("p (t m j) -> p m j t", t=PACK, j=PACK)
            src = w1_raw[a][:].rearrange("p j (m t) -> p m j t", t=PACK)
            if a >= last - 1:
                nc.vector.tensor_copy(out=dst[:, :, :, 0:2], in_=src[:, :, :, 0:2])
                nc.scalar.copy(out=dst[:, :, :, 2:4], in_=src[:, :, :, 2:4])
                for half in range(2):
                    cols = slice(half * (H // 2), (half + 1) * (H // 2))
                    wide = slice(half * PACK * (H // 2), (half + 1) * PACK * (H // 2))
                    nc.vector.quantize_mx(out=w1_codes[a][:, cols].bitcast(FP8X4), scales=w1_scales[a][:, cols], in_=woven[:, wide])
            else:
                nc.scalar.copy(out=dst[:, :, :, 0:2], in_=src[:, :, :, 0:2])
                nc.scalar.copy(out=dst[:, :, :, 2:4], in_=src[:, :, :, 2:4])
                nc.vector.quantize_mx(out=w1_codes[a][:].bitcast(FP8X4), scales=w1_scales[a][:], in_=woven[:])

        got_scales = keep.tile([P, S], U8, name="got_scales", align_bytes=64)
        h_banks = [psum.tile([P, PACK, SLICE], F32, name=f"h{s}", tag=f"bank{s}") for s in range(SLICES)]

        def first_product(a, s):
            for t in range(PACK):
                cols = slice(t * P, (t + 1) * P)
                nc.tensor.matmul_mx(
                    out=h_banks[s][:, t, :],
                    lhsT=w1_codes[a][:, cols].bitcast(FP8X4),
                    lhsT_scale=w1_scales[a][:, cols],
                    rhs=picked[(a, s)].bitcast(FP8X4),
                    rhs_scale=got_scales[4 * a : P, s * SLICE : (s + 1) * SLICE],
                    start=(a == 0 and t == 0),
                    stop=(a == last and t == PACK - 1),
                )

        for a in range(last):
            for half in range(2):
                gather_words(a, half * (S // 2), S // 2)
            if a == 0:
                nc.vector.tensor_copy(got_scales[:], tab_scales[:].indirect(pick[:]))
            quantise_w1(a)
            for s in range(SLICES):
                first_product(a, s)
        quantise_w1(last)
        for j0 in range(0, S - 2 * SLICE, 2 * SLICE):
            gather_words(last, j0, 2 * SLICE)

        groups = [(0, 1), (1, 2), (2, 4), (4, 8)]
        h_bf = {}
        h_codes = {}
        h_scales = {}
        for s0, s1 in groups:
            n = (s1 - s0) * SLICE
            h_bf[s0] = keep.tile([P, PACK * n], BF16, name=f"h_bf{s0}", tag=f"h_bf{s0}", align_bytes=64)
            h_codes[s0] = keep.tile([P, n], U32, name=f"h_codes{s0}", align_bytes=64)
            h_scales[s0] = keep.tile([P, n], U8, name=f"h_scales{s0}", align_bytes=64)

        def relu(s0, s):
            first_product(last, s)
            lo = (s - s0) * PACK * SLICE
            dst = h_bf[s0][:, lo : lo + PACK * SLICE].rearrange("p (n t) -> p n t", t=PACK)
            nc.scalar.activation(out=dst, in_=h_banks[s][:].rearrange("p t n -> p n t"), func=ACT.Relu)

        def quantise_h(s0):
            nc.vector.quantize_mx(out=h_codes[s0][:].bitcast(FP8X4), scales=h_scales[s0][:], in_=h_bf[s0][:])

        def second_product(c, lo, hi, bank):
            y = psum.tile([P, (hi - lo) * SLICE], F32, name=f"y{c}_{lo}", tag=f"bank{bank}")
            for s0, s1 in groups:
                if lo <= s0 and s1 <= hi:
                    nc.tensor.matmul_mx(
                        out=y[:, (s0 - lo) * SLICE : (s1 - lo) * SLICE],
                        lhsT=w2w[:, 2 * P * c : 2 * P * (c + 1)].bitcast(FP4X4),
                        lhsT_scale=w2s[:, P * c : P * (c + 1)],
                        rhs=h_codes[s0][:].bitcast(FP8X4),
                        rhs_scale=h_scales[s0][:],
                        start=True,
                        stop=True,
                    )
            return y

        def put(c, lo, hi, y):
            j0, j1 = lo * SLICE, hi * SLICE
            act = keep.tile([P, j1 - j0], F32, name=f"act{c}_{lo}")
            nc.scalar.activation(out=act[:], in_=y[:], func=ACT.Gelu_apprx_tanh, bias=bias[:, c : c + 1])
            window = pages[c][:].indirect(place[:, j0 // PER_COL : j1 // PER_COL])
            nc.vector.tensor_tensor(window, act[:], gain[:, j0:j1], MULT)

        relu(0, 0)
        quantise_h(0)
        gather_words(last, S - 2 * SLICE, 2 * SLICE, tag="h_bf0")
        relu(1, 1)
        quantise_h(1)
        y = second_product(0, 0, 1, 0)
        relu(2, 2)
        put(0, 0, 1, y)
        relu(2, 3)
        quantise_h(2)
        put(1, 0, 2, second_product(1, 0, 2, 3))
        put(0, 1, 4, second_product(0, 1, 4, 2))
        for s in range(4, 8):
            relu(4, s)
        quantise_h(4)
        put(1, 2, 4, second_product(1, 2, 4, 7))
        for c in range(2):
            put(c, 4, 8, second_product(c, 4, 8, 4 + c))
            nc.sync.dma_start(out=out[c * P : (c + 1) * P, :], in_=pages[c][:])
